import numpy as np
import ml_dtypes

BF16 = ml_dtypes.bfloat16


def bf(x):
    return np.asarray(x, np.float32).astype(BF16)


def f32(x):
    return np.asarray(x, np.float32)


def f64(x):
    return np.asarray(x).astype(np.float64)


def striped(idx):
    return np.tile(idx.reshape(-1, 16).T, (8, 1))


def rows(idx, k):
    return np.tile(idx, (k, 1))


def look(tab, idx):
    return np.take_along_axis(f64(tab), rows(idx, len(tab)), axis=1)


K, S, V, N, M = 256, 256, 256, 256, 128


def setup_inputs():
    return {"tab": f32(np.random.standard_normal((K, S))), "qry": f32(np.random.standard_normal((K, V))), "w": bf(np.random.uniform(0.0, 1.0, (K, M)) / K), "offs": striped(np.random.randint(0, S, N))}


def reference(tab, qry, w, offs):
    idx = offs[:16].T.reshape(-1)
    x = np.abs(look(tab, idx) - f64(qry))
    y = f64(w).T @ x
    return np.exp(-y)

@@ -1,0 +1,52 @@
+import concourse.mybir as mybir
+
+BF16, F32, U16 = mybir.dt.bfloat16, mybir.dt.float32, mybir.dt.uint16
+SUBTRACT = mybir.AluOpType.subtract
+ABS, EXP = mybir.ActivationFunctionType.Abs, mybir.ActivationFunctionType.Exp
+
+P = 128
+DIMS = 256
+BLOCKS = DIMS // P
+COLUMNS = 256
+QUERIES = 256
+METRICS = 128
+STRIPE = 16
+PIECE = 128
+PIECES = QUERIES // PIECE
+
+FLOPS = 2 * DIMS * METRICS * QUERIES + 2 * DIMS * QUERIES
+
+
+def tile_lookup_manh_sub_rbf_kernel(tc, tab, qry, w, offs, out):
+    nc = tc.nc
+    with (
+        tc.tile_pool(name="held", bufs=1) as held,
+        tc.psum_pool(name="psum", bufs=1) as psum,
+    ):
+        offsets = held.tile([P, QUERIES // STRIPE], U16, name="offsets")
+        nc.sync.dma_start(offsets[:], offs)
+        tables = [held.tile([P, COLUMNS], F32, name=f"table{b}") for b in range(BLOCKS)]
+        queries = [held.tile([P, QUERIES], F32, name=f"queries{b}") for b in range(BLOCKS)]
+        weights = held.tile([P, BLOCKS, METRICS], BF16, name="weights")
+        for b in range(BLOCKS):
+            nc.sync.dma_start(tables[b][:], tab[b * P : (b + 1) * P, :])
+            nc.sync.dma_start(queries[b][:], qry[b * P : (b + 1) * P, :])
+        nc.sync.dma_start(weights[:], w.rearrange("(b p) m -> p b m", p=P))
+
+        for piece in range(PIECES):
+            columns = slice(piece * PIECE, (piece + 1) * PIECE)
+            stripe = slice(piece * PIECE // STRIPE, (piece + 1) * PIECE // STRIPE)
+            sums = psum.tile([METRICS, PIECE], F32, name=f"sums{piece}")
+            for b in range(BLOCKS):
+                difference = held.tile([P, PIECE], F32, name=f"difference{piece}_{b}")
+                nc.vector.tensor_tensor(
+                    difference[:], tables[b][:].indirect(offsets[:, stripe]), queries[b][:, columns], SUBTRACT
+                )
+                magnitude = held.tile([P, PIECE], BF16, name=f"magnitude{piece}_{b}")
+                nc.scalar.activation(magnitude[:], difference[:], ABS)
+                nc.tensor.matmul(
+                    sums[:], weights[:, b, :], magnitude[:], start=(b == 0), stop=(b == BLOCKS - 1)
+                )
+            kernel_values = held.tile([METRICS, PIECE], F32, name=f"kernel_values{piece}")
+            nc.scalar.activation(kernel_values[:], sums[:], EXP, scale=-1.0)
+            nc.sync.dma_start(out[:, columns], kernel_values[:])

@@ -19,6 +19,7 @@ FLOPS = 2 * DIMS * METRICS * QUERIES + 2 * DIMS * QUERIES
 
 def tile_lookup_manh_sub_rbf_kernel(tc, tab, qry, w, offs, out):
     nc = tc.nc
+    piece_columns = [slice(piece * PIECE, (piece + 1) * PIECE) for piece in range(PIECES)]
     with (
         tc.tile_pool(name="held", bufs=1) as held,
         tc.psum_pool(name="psum", bufs=1) as psum,
@@ -33,20 +34,20 @@ def tile_lookup_manh_sub_rbf_kernel(tc, tab, qry, w, offs, out):
             nc.sync.dma_start(queries[b][:], qry[b * P : (b + 1) * P, :])
         nc.sync.dma_start(weights[:], w.rearrange("(b p) m -> p b m", p=P))
 
-        for piece in range(PIECES):
-            columns = slice(piece * PIECE, (piece + 1) * PIECE)
-            stripe = slice(piece * PIECE // STRIPE, (piece + 1) * PIECE // STRIPE)
-            sums = psum.tile([METRICS, PIECE], F32, name=f"sums{piece}")
-            for b in range(BLOCKS):
-                difference = held.tile([P, PIECE], F32, name=f"difference{piece}_{b}")
+        sums = [psum.tile([METRICS, PIECE], F32, name=f"sums{piece}") for piece in range(PIECES)]
+        for b in range(BLOCKS):
+            for piece, columns in enumerate(piece_columns):
+                stripe = slice(piece * PIECE // STRIPE, (piece + 1) * PIECE // STRIPE)
+                difference = held.tile([P, PIECE], F32, name=f"difference{b}_{piece}")
                 nc.vector.tensor_tensor(
                     difference[:], tables[b][:].indirect(offsets[:, stripe]), queries[b][:, columns], SUBTRACT
                 )
-                magnitude = held.tile([P, PIECE], BF16, name=f"magnitude{piece}_{b}")
+                magnitude = held.tile([P, PIECE], BF16, name=f"magnitude{b}_{piece}")
                 nc.scalar.activation(magnitude[:], difference[:], ABS)
                 nc.tensor.matmul(
-                    sums[:], weights[:, b, :], magnitude[:], start=(b == 0), stop=(b == BLOCKS - 1)
+                    sums[piece][:], weights[:, b, :], magnitude[:], start=(b == 0), stop=(b == BLOCKS - 1)
                 )
+        for piece, columns in enumerate(piece_columns):
             kernel_values = held.tile([METRICS, PIECE], F32, name=f"kernel_values{piece}")
-            nc.scalar.activation(kernel_values[:], sums[:], EXP, scale=-1.0)
+            nc.scalar.activation(kernel_values[:], sums[piece][:], EXP, scale=-1.0)
             nc.sync.dma_start(out[:, columns], kernel_values[:])

import concourse.mybir as mybir

BF16, F32, U16 = mybir.dt.bfloat16, mybir.dt.float32, mybir.dt.uint16
SUBTRACT = mybir.AluOpType.subtract
ABS, EXP = mybir.ActivationFunctionType.Abs, mybir.ActivationFunctionType.Exp

P = 128
DIMS = 256
BLOCKS = DIMS // P
COLUMNS = 256
QUERIES = 256
METRICS = 128
STRIPE = 16
PIECE = 128
PIECES = QUERIES // PIECE

FLOPS = 2 * DIMS * METRICS * QUERIES + 2 * DIMS * QUERIES


def tile_lookup_manh_sub_rbf_kernel(tc, tab, qry, w, offs, out):
    nc = tc.nc
    piece_columns = [slice(piece * PIECE, (piece + 1) * PIECE) for piece in range(PIECES)]
    with (
        tc.tile_pool(name="held", bufs=1) as held,
        tc.psum_pool(name="psum", bufs=1) as psum,
    ):
        offsets = held.tile([P, QUERIES // STRIPE], U16, name="offsets")
        nc.sync.dma_start(offsets[:], offs)
        tables = [held.tile([P, COLUMNS], F32, name=f"table{b}") for b in range(BLOCKS)]
        queries = [held.tile([P, QUERIES], F32, name=f"queries{b}") for b in range(BLOCKS)]
        weights = held.tile([P, BLOCKS, METRICS], BF16, name="weights")
        for b in range(BLOCKS):
            nc.sync.dma_start(tables[b][:], tab[b * P : (b + 1) * P, :])
            nc.sync.dma_start(queries[b][:], qry[b * P : (b + 1) * P, :])
        nc.sync.dma_start(weights[:], w.rearrange("(b p) m -> p b m", p=P))

        sums = [psum.tile([METRICS, PIECE], F32, name=f"sums{piece}") for piece in range(PIECES)]
        for b in range(BLOCKS):
            for piece, columns in enumerate(piece_columns):
                stripe = slice(piece * PIECE // STRIPE, (piece + 1) * PIECE // STRIPE)
                difference = held.tile([P, PIECE], F32, name=f"difference{b}_{piece}")
                nc.vector.tensor_tensor(
                    difference[:], tables[b][:].indirect(offsets[:, stripe]), queries[b][:, columns], SUBTRACT
                )
                magnitude = held.tile([P, PIECE], BF16, name=f"magnitude{b}_{piece}")
                nc.scalar.activation(magnitude[:], difference[:], ABS)
                nc.tensor.matmul(
                    sums[piece][:], weights[:, b, :], magnitude[:], start=(b == 0), stop=(b == BLOCKS - 1)
                )
        for piece, columns in enumerate(piece_columns):
            kernel_values = held.tile([METRICS, PIECE], F32, name=f"kernel_values{piece}")
            nc.scalar.activation(kernel_values[:], sums[piece][:], EXP, scale=-1.0)
            nc.sync.dma_start(out[:, columns], kernel_values[:])
